import numpy as np
import ml_dtypes


def mxq(x, axis, fmt="e4m3"):
    dtype, down = {"e4m3": (ml_dtypes.float8_e4m3fn, 7), "e5m2": (ml_dtypes.float8_e5m2, 14)}[fmt]
    v = np.moveaxis(np.asarray(x, np.float32).astype(ml_dtypes.bfloat16).astype(np.float64), axis, -1)
    blocks = v.reshape(v.shape[:-1] + (-1, 32))
    amax = np.abs(blocks).max(-1, keepdims=True)
    byte = np.maximum(np.where(amax > 0, np.frexp(amax)[1] - 1 + 127, 0) - down, 1)
    scale = np.exp2(byte - 127.0)
    codes = (blocks / scale).astype(np.float32).astype(dtype).astype(np.float64)
    return np.moveaxis((codes * scale).reshape(v.shape), -1, axis)


WIDE = False


def mx_kscale(k):
    if not WIDE:
        return np.ones(k)
    levels = np.array([10, -10, 5, -5, 0])
    if k % 512:
        return np.exp2(np.random.permutation(np.resize(levels, k // 32))).repeat(32)
    a = np.empty((k // 512, 16))
    for p in range(k // 512):
        a[p, :8] = np.random.permutation(np.resize(levels, 8))
        for g in range(8):
            far = levels[np.abs(levels - a[p, g]) >= 10]
            a[p, g + 8] = far[np.random.randint(len(far))]
    return np.exp2(a.ravel()).repeat(32)


BF16 = ml_dtypes.bfloat16


def bf(x):
    return np.asarray(x, np.float32).astype(BF16)


def f64(x):
    return np.asarray(x).astype(np.float64)


E2M1 = np.array([0.0, 0.5, 1.0, 1.5, 2.0, 3.0, 4.0, 6.0, -0.0, -0.5, -1.0, -1.5, -2.0, -3.0, -4.0, -6.0])


def pack_weight(w, fmt):
    k, n = w.shape
    w = f64(bf(w)).reshape(k // 32, 32, n)
    amax = np.abs(w).max(1)
    if fmt == "e4m3":
        byte = np.frexp(amax)[1] - 1 + 127 - 7
    else:
        mant, ex = np.frexp(amax / 6.0)
        byte = np.where(mant > 0.5, ex, ex - 1) + 127
    byte = np.clip(np.where(amax > 0, byte, 1), 1, 254)
    scaled = (w * np.exp2(127.0 - byte)[:, None, :]).reshape(k, n).astype(np.float32)
    by_word = np.ascontiguousarray(scaled.reshape(k // 512, 128, 4, n).transpose(0, 1, 3, 2))
    if fmt == "e4m3":
        words = by_word.astype(ml_dtypes.float8_e4m3fn).view(np.uint8)
    else:
        c = by_word.astype(ml_dtypes.float4_e2m1fn).view(np.uint8) & 0xF
        words = c[..., 0::2] | (c[..., 1::2] << 4)
    return np.ascontiguousarray(words), np.ascontiguousarray(byte.astype(np.uint8).reshape(k // 512, 16, n))


def unpack_weight(words, scales, fmt):
    g, p, n, _ = words.shape
    if fmt == "e4m3":
        vals = np.ascontiguousarray(words).view(ml_dtypes.float8_e4m3fn).astype(np.float64)
    else:
        nib = np.empty((g, p, n, 4), np.uint8)
        nib[..., 0::2] = words & 0xF
        nib[..., 1::2] = words >> 4
        vals = E2M1[nib]
    vals = vals * np.repeat(np.exp2(scales.astype(np.float64) - 127.0), 8, axis=1)[..., None]
    return vals.transpose(0, 1, 3, 2).reshape(g * 512, n)
def pack4(w):
    words, scales = pack_weight(w, "e2m1")
    return words.reshape(words.shape[0], 128, -1), scales


def unpack4(words, scales):
    return unpack_weight(words.reshape(words.shape[0], 128, -1, 2), scales, "e2m1")


def planes(Y):
    n, m = Y.shape
    b = f64(bf(Y)).reshape(n // 32, 32, m)
    amax = np.abs(b).max(1)
    byte = np.clip(np.where(amax > 0, np.frexp(amax)[1] - 1 + 127 - 7, 1), 1, 254)
    codes = (b * np.exp2(127.0 - byte)[:, None, :]).reshape(n, m).astype(np.float32).astype(ml_dtypes.float8_e4m3fn).view(np.uint8)
    words = codes.reshape(n // 512, 128, 4, m).transpose(0, 1, 3, 2)
    return np.ascontiguousarray(words), np.ascontiguousarray(byte.astype(np.uint8).reshape(n // 512, 16, m))


IH, IW, GY, GX, D, R, P, K, N = 48, 32, 4, 8, 32, 4, 1536, 1024, 1024

SIG = 2.0 / np.sqrt(GY * GX * R)


def hat(v, cells, half):
    return np.maximum(0.0, 1.0 - np.abs(v[:, None] - np.arange(cells)) / half)


def setup_inputs():
    t = mx_kscale(K)
    row, col = np.repeat(np.arange(IH), IW), np.tile(np.arange(IW), IH)
    hy = hat(row * (GY - 1) / (IH - 1), GY, GY)
    hx = hat(col * (GX - 1) / (IW - 1), GX, GX)
    hd = hat((D - 1) * np.random.rand(P), D, R)
    w = (hy[:, :, None, None] * hx[:, None, :, None] * hd[:, None, None, :]).reshape(P, K)
    h_words, h_scales = pack_weight((w * t).T, "e4m3")
    size = SIG * np.exp(0.7 * np.random.randn(N))
    a_words, a_scales = pack4(np.random.randn(K, N) * size / t[:, None])
    b_words, b_scales = pack_weight(np.random.randn(K, N) * size / t[:, None], "e4m3")
    c_grid = bf(np.random.randn(K, N) * size / t[:, None])
    return {"h_words": h_words, "h_scales": h_scales, "a_words": a_words, "a_scales": a_scales,
            "b_words": b_words, "b_scales": b_scales, "c_grid": c_grid,
            "x": bf(np.random.randn(P, N)), "u": bf(np.random.randn(P, N))}


def reference(h_words, h_scales, a_words, a_scales, b_words, b_scales, c_grid, x, u):
    H = unpack_weight(h_words, h_scales, "e4m3")
    sx = H.T @ unpack4(a_words, a_scales)
    su = H.T @ mxq(f64(c_grid), 0, "e4m3")
    bias = H.T @ unpack_weight(b_words, b_scales, "e4m3")
    y = sx * f64(x) + su * f64(u) + bias
    Y = y.T
    words, scales = planes(Y)
    return y, words, scales

@@ -1,0 +1,346 @@
+from contextlib import ExitStack
+
+import concourse.mybir as mybir
+from concourse.masks import make_identity
+
+PIXELS, CELLS, CHANNELS = 1536, 1024, 1024
+FLOPS = 2 * 3 * PIXELS * CELLS * CHANNELS
+
+F32 = mybir.dt.float32
+BF16 = mybir.dt.bfloat16
+I32 = mybir.dt.int32
+U32 = mybir.dt.uint32
+U8 = mybir.dt.uint8
+FP8X4 = mybir.dt.float8_e4m3fn_x4
+FP4X4 = mybir.dt.float4_e2m1fn_x4
+MULT = mybir.AluOpType.mult
+ADD = mybir.AluOpType.add
+
+P = 128
+PASSES = CELLS // 512
+HALF = 512
+TILES = PIXELS // P
+UNITS = 2 * TILES
+PAIRS = UNITS // 2
+B_ROW = 4
+
+
+def tile_bilateral_grid_affine_k3_kernel(
+    tc, h_words, h_scales, a_words, a_scales, b_words, b_scales, c_grid, x, u, out_0, out_1, out_2
+):
+    nc = tc.nc
+    with ExitStack() as ctx:
+        keep = ctx.enter_context(tc.tile_pool(name="keep", bufs=1))
+        work = ctx.enter_context(tc.tile_pool(name="work", bufs=1))
+        psum = ctx.enter_context(tc.psum_pool(name="psum", bufs=1))
+        ctx.enter_context(tc.manual_schedule())
+
+        h_plane = keep.tile([P, PASSES, PIXELS], U8, name="h_plane", align_bytes=64)
+        a_plane = keep.tile([P, PASSES, CHANNELS], U8, name="a_plane", align_bytes=64)
+        b_plane = keep.tile([P, PASSES, CHANNELS], U8, name="b_plane", align_bytes=64)
+        for plane in (h_plane, a_plane, b_plane):
+            nc.vector.memset(plane[:].bitcast(I32), 0)
+
+        ident = keep.tile([P, P], F32, name="ident")
+        make_identity(nc, ident[:])
+
+        h_rows = h_words.rearrange("g p n t -> p g (n t)")
+        a_rows = a_words.rearrange("g p n -> p g n")
+        b_rows = b_words.rearrange("g p n t -> p g (n t)")
+        h_of, x_of, u_of = {}, {}, {}
+        a_of, b_of, c_raw = {}, {}, {}
+
+        def load_plane(plane, scales, first_row):
+            for r in range(4):
+                nc.sync.dma_start(
+                    out=plane[first_row + r : P : 32, :, :].bitcast(I32),
+                    in_=scales[:, r:16:4, :].rearrange("g q n -> q g n").bitcast(I32),
+                )
+
+        def load_h(first, count):
+            codes = keep.tile([P, PASSES, count * P], U32, name="h%d" % first, align_bytes=64)
+            nc.sync.dma_start(
+                out=codes[:].bitcast(I32),
+                in_=h_rows[:, :, 4 * P * first : 4 * P * (first + count)].bitcast(I32),
+            )
+            for i in range(count):
+                h_of[first + i] = (codes, i)
+
+        def load_a(half):
+            codes = keep.tile([P, PASSES, 2 * HALF], U8, name="a%d" % half, align_bytes=64)
+            nc.sync.dma_start(
+                out=codes[:].bitcast(I32),
+                in_=a_rows[:, :, 2 * HALF * half : 2 * HALF * (half + 1)].bitcast(I32),
+            )
+            a_of[half] = codes
+
+        def load_b(half):
+            codes = keep.tile([P, PASSES, HALF], U32, name="b%d" % half, align_bytes=64)
+            nc.sync.dma_start(
+                out=codes[:].bitcast(I32),
+                in_=b_rows[:, :, 4 * HALF * half : 4 * HALF * (half + 1)].bitcast(I32),
+            )
+            b_of[half] = codes
+
+        def load_c(half, g):
+            raw = keep.tile([P, 4, HALF], BF16, name="c_raw%d%d" % (half, g))
+            nc.sync.dma_start(
+                out=raw[:],
+                in_=c_grid[512 * g : 512 * (g + 1), HALF * half : HALF * (half + 1)].rearrange(
+                    "(p t) n -> p t n", t=4
+                ),
+            )
+            c_raw[half, g] = raw
+
+        def load_image(image, name, store, half, first, count):
+            rows = keep.tile([P, count, HALF], BF16, name="%s%d_%d" % (name, half, first))
+            nc.sync.dma_start(
+                out=rows[:],
+                in_=image[P * first : P * (first + count), HALF * half : HALF * (half + 1)].rearrange(
+                    "(i p) n -> p i n", p=P
+                ),
+            )
+            for i in range(count):
+                store[TILES * half + first + i] = rows[:, i, :]
+
+        def load_x(half, first, count):
+            load_image(x, "x", x_of, half, first, count)
+
+        def load_u(half, first, count):
+            load_image(u, "u", u_of, half, first, count)
+
+        load_h(0, 2)
+        load_a(0)
+        load_plane(h_plane, h_scales, 0)
+        load_plane(a_plane, a_scales, 0)
+        load_b(0)
+        load_x(0, 0, 2)
+        load_plane(b_plane, b_scales, B_ROW)
+        load_h(2, 2)
+        load_x(0, 2, 2)
+        load_c(0, 0)
+        load_h(4, 2)
+        load_x(0, 4, 2)
+        load_c(0, 1)
+        load_h(6, 2)
+        load_x(0, 6, 2)
+        load_u(0, 0, 4)
+        load_h(8, 4)
+        load_x(0, 8, 4)
+        load_u(0, 4, 4)
+        load_c(1, 0)
+        load_c(1, 1)
+        load_a(1)
+        load_b(1)
+        load_x(1, 0, 4)
+        load_u(0, 8, 4)
+        for first in range(0, TILES, 4):
+            if first > 0:
+                load_x(1, first, 4)
+            load_u(1, first, 4)
+
+        c_lined, c_codes, c_plane = {}, {}, {}
+        for half in range(2):
+            c_lined[half] = keep.tile([P, PASSES, HALF, 4], BF16, name="c_lined%d" % half, align_bytes=64)
+            c_codes[half] = keep.tile([P, PASSES, HALF], U32, name="c_codes%d" % half, align_bytes=64)
+            c_plane[half] = keep.tile([P, PASSES, HALF], U8, name="c_plane%d" % half, align_bytes=64)
+        y_of = [keep.tile([P, 2, HALF], F32, name="y%d" % pair) for pair in range(PAIRS)]
+        y_plane = [keep.tile([P, PIXELS], U8, name="y_plane%d" % half, align_bytes=64) for half in range(2)]
+        ux_of, yb_of = {}, {}
+
+        def line_up_c_scalar(half, g, cols):
+            nc.scalar.copy(
+                out=c_lined[half][:, g, cols, :].rearrange("p (c i) t -> p c t i", i=4),
+                in_=c_raw[half, g][:, :, cols].rearrange("p t (c i) -> p c t i", i=4),
+            )
+
+        def line_up_c_gpsimd(half, g, cols):
+            nc.gpsimd.tensor_scalar(
+                out=c_lined[half][:, g, cols, :],
+                in0=c_raw[half, g][:, :, cols].rearrange("p t c -> p c t"),
+                scalar1=1.0,
+                scalar2=0.0,
+                op0=MULT,
+                op1=ADD,
+            )
+
+        def quantize_c(half, passes):
+            nc.vector.quantize_mx(
+                out=c_codes[half][:, passes, :].rearrange("p g n -> p (g n)").bitcast(FP8X4),
+                scales=c_plane[half][:, passes, :].rearrange("p g n -> p (g n)"),
+                in_=c_lined[half][:, passes, :, :].rearrange("p g n t -> p (g n t)"),
+            )
+
+        def slice_grid(unit, codes_of_pass, plane_of_pass):
+            tile_no = unit % TILES
+            h_codes, i = h_of[tile_no]
+            acc = psum.tile([P, HALF], F32, name="acc", bufs=6)
+            for g in range(PASSES):
+                nc.tensor.matmul_mx(
+                    out=acc[:],
+                    lhsT=h_codes[:, g, P * i : P * (i + 1)].bitcast(FP8X4),
+                    lhsT_scale=h_plane[:, g, P * tile_no : P * (tile_no + 1)],
+                    rhs=codes_of_pass(g),
+                    rhs_scale=plane_of_pass(g),
+                    start=(g == 0),
+                    stop=(g == PASSES - 1),
+                )
+            return acc
+
+        def job_a(unit):
+            half = unit // TILES
+            cols = slice(HALF * half, HALF * (half + 1))
+            acc = slice_grid(unit, lambda g: a_of[half][:, g, :].bitcast(FP4X4), lambda g: a_plane[:, g, cols])
+            nc.vector.tensor_tensor(out=y_of[unit // 2][:, unit % 2, :], in0=acc[:], in1=x_of[unit], op=MULT)
+
+        def job_b(unit):
+            half = unit // TILES
+            cols = slice(HALF * half, HALF * (half + 1))
+            acc = slice_grid(
+                unit, lambda g: b_of[half][:, g, :].bitcast(FP8X4), lambda g: b_plane[B_ROW:P, g, cols]
+            )
+            y = y_of[unit // 2][:, unit % 2, :]
+            nc.vector.tensor_tensor(out=y, in0=acc[:], in1=y, op=ADD)
+
+        def job_c(unit):
+            half = unit // TILES
+            if unit % 2 == 0:
+                ux_of[unit // 2] = work.tile([P, 2, HALF], F32, name="su_u", bufs=3)
+            acc = slice_grid(unit, lambda g: c_codes[half][:, g, :].bitcast(FP8X4), lambda g: c_plane[half][:, g, :])
+            nc.vector.tensor_tensor(out=ux_of[unit // 2][:, unit % 2, :], in0=acc[:], in1=u_of[unit], op=MULT)
+
+        def finish_pair(pair):
+            y = y_of[pair][:].rearrange("p i n -> p (i n)")
+            nc.gpsimd.tensor_tensor(out=y, in0=y, in1=ux_of[pair][:].rearrange("p i n -> p (i n)"), op=ADD)
+
+        def store_y(pair, members):
+            half, first = divmod(2 * pair, TILES)
+            rows = out_0[P * first : P * (first + 2), HALF * half : HALF * (half + 1)].rearrange(
+                "(i p) n -> p i n", p=P
+            )
+            nc.sync.dma_start(out=rows[:, members, :], in_=y_of[pair][:, members, :])
+
+        def round_y(pair, members):
+            if members.start == 0:
+                yb_of[pair] = work.tile([P, 2, HALF], BF16, name="y_bf16", bufs=4)
+            for i in range(members.start, members.stop):
+                nc.scalar.copy(
+                    out=yb_of[pair][:, i, :].rearrange("x (w p e) -> x w p e", w=2, e=2),
+                    in_=y_of[pair][:, i, :].rearrange("x (p w e) -> x w p e", w=2, e=2),
+                )
+
+        def turn(pair):
+            bank = psum.tile([P, 2, 2, P], F32, name="turned", bufs=2)
+            words = yb_of[pair][:].bitcast(F32)
+            for i in range(2):
+                for w in range(2):
+                    nc.tensor.transpose(bank[:, i, w, :], words[:, i, P * w : P * (w + 1)], ident[:])
+            return bank
+
+        def empty_bank(bank, lined, copy):
+            copy(
+                out=lined.bitcast(F32).rearrange("p (i m w) -> p i m w", i=2, w=2),
+                in_=bank[:].rearrange("p i w m -> p i m w"),
+            )
+
+        def quantize_y(lined, first_pair, pairs):
+            half, first = divmod(2 * first_pair, TILES)
+            width = 2 * P * pairs
+            codes = keep.tile([P, width], U32, name="y_codes%d" % first_pair, align_bytes=64)
+            nc.vector.quantize_mx(
+                out=codes[:].bitcast(FP8X4),
+                scales=y_plane[half][:, P * first : P * first + width],
+                in_=lined,
+            )
+            nc.sync.dma_start(
+                out=out_1[half].rearrange("p m t -> p (m t)")[:, 4 * P * first : 4 * (P * first + width)].bitcast(I32),
+                in_=codes[:].bitcast(I32),
+            )
+
+        def store_plane(half):
+            for r in range(4):
+                nc.sync.dma_start(
+                    out=out_2[half, r:16:4, :].bitcast(I32), in_=y_plane[half][r:P:32, :].bitcast(I32)
+                )
+
+        left, right = slice(0, HALF // 2), slice(HALF // 2, HALF)
+        both = slice(0, 2)
+
+        for g in range(PASSES):
+            line_up_c_scalar(0, g, left)
+            line_up_c_gpsimd(0, g, right)
+        for pair in range(3):
+            job_a(2 * pair)
+            job_a(2 * pair + 1)
+            if pair == 2:
+                quantize_c(0, slice(0, 1))
+            job_b(2 * pair)
+            job_b(2 * pair + 1)
+        quantize_c(0, slice(1, 2))
+
+        ahead = 6
+        banks = []
+        lined = None
+        for pair in range(PAIRS - 1):
+            group_due = pair >= 4 and pair % 2 == 0
+            if group_due:
+                lined = work.tile([P, 2, 4 * 2 * P], BF16, name="y_lined", bufs=2, align_bytes=64)
+                for j in range(2):
+                    empty_bank(banks[j], lined[:, j, :], nc.scalar.copy)
+            if 2 <= pair <= 5:
+                g, side = divmod(pair - 2, 2)
+                line_up_c_scalar(1, g, (left, right)[side])
+            if pair >= 1:
+                round_y(pair - 1, both)
+                store_y(pair - 1, both)
+            if group_due or pair == 5:
+                job_a(ahead)
+                job_a(ahead + 1)
+                job_b(ahead)
+                job_b(ahead + 1)
+                ahead = ahead + 2
+                job_c(2 * pair)
+                if group_due:
+                    quantize_y(lined[:].rearrange("p j n -> p (j n)"), pair - 4, 2)
+                    if pair == 8:
+                        store_plane(0)
+                else:
+                    quantize_c(1, both)
+            else:
+                job_a(ahead)
+                job_c(2 * pair)
+                job_b(ahead)
+                ahead = ahead + 1
+            job_c(2 * pair + 1)
+            finish_pair(pair)
+            if pair >= 3 and pair % 2 == 1:
+                banks = [turn(pair - 3), turn(pair - 2)]
+
+        last = PAIRS - 1
+        job_a(2 * last)
+        job_a(2 * last + 1)
+        banks = [turn(last - 3), turn(last - 2)]
+        lined = work.tile([P, 2, 4 * 2 * P], BF16, name="y_lined", bufs=2, align_bytes=64)
+        for j in range(2):
+            empty_bank(banks[j], lined[:, j, :], nc.scalar.copy)
+        round_y(last - 1, both)
+        store_y(last - 1, both)
+        job_b(2 * last)
+        job_b(2 * last + 1)
+        job_c(2 * last)
+        job_c(2 * last + 1)
+        bank_before = turn(last - 1)
+        for i in range(2):
+            y = y_of[last][:, i, :]
+            nc.vector.tensor_tensor(out=y, in0=y, in1=ux_of[last][:, i, :], op=ADD)
+            round_y(last, slice(i, i + 1))
+            store_y(last, slice(i, i + 1))
+        bank_last = turn(last)
+        lined_before = work.tile([P, 4 * 2 * P], BF16, name="lined_before", align_bytes=64)
+        lined_last = work.tile([P, 4 * 2 * P], BF16, name="lined_last", align_bytes=64)
+        empty_bank(bank_before, lined_before[:], nc.vector.tensor_copy)
+        empty_bank(bank_last, lined_last[:], nc.scalar.copy)
+        quantize_y(lined[:].rearrange("p j n -> p (j n)"), last - 3, 2)
+        quantize_y(lined_before[:], last - 1, 1)
+        quantize_y(lined_last[:], last, 1)
+        store_plane(1)

@@ -23,6 +23,7 @@ TILES = PIXELS // P
 UNITS = 2 * TILES
 PAIRS = UNITS // 2
 B_ROW = 4
+H_FIRST = 6 * P
 
 
 def tile_bilateral_grid_affine_k3_kernel(
@@ -35,14 +36,12 @@ def tile_bilateral_grid_affine_k3_kernel(
         psum = ctx.enter_context(tc.psum_pool(name="psum", bufs=1))
         ctx.enter_context(tc.manual_schedule())
 
-        h_plane = keep.tile([P, PASSES, PIXELS], U8, name="h_plane", align_bytes=64)
-        a_plane = keep.tile([P, PASSES, CHANNELS], U8, name="a_plane", align_bytes=64)
+        h_plane_first = keep.tile([P, PASSES, H_FIRST], U8, name="h_plane_first", align_bytes=64)
+        h_plane_rest = keep.tile([P, PASSES, PIXELS - H_FIRST], U8, name="h_plane_rest", align_bytes=64)
+        a_plane = [keep.tile([P, PASSES, HALF], U8, name="a_plane%d" % h, align_bytes=64) for h in range(2)]
         b_plane = keep.tile([P, PASSES, CHANNELS], U8, name="b_plane", align_bytes=64)
-        for plane in (h_plane, a_plane, b_plane):
+        for plane in (h_plane_first, b_plane, a_plane[0], h_plane_rest, a_plane[1]):
             nc.vector.memset(plane[:].bitcast(I32), 0)
-
-        ident = keep.tile([P, P], F32, name="ident")
-        make_identity(nc, ident[:])
 
         h_rows = h_words.rearrange("g p n t -> p g (n t)")
         a_rows = a_words.rearrange("g p n -> p g n")
@@ -50,9 +49,9 @@ def tile_bilateral_grid_affine_k3_kernel(
         h_of, x_of, u_of = {}, {}, {}
         a_of, b_of, c_raw = {}, {}, {}
 
-        def load_plane(plane, scales, first_row):
+        def load_plane(queue, plane, scales, first_row):
             for r in range(4):
-                nc.sync.dma_start(
+                queue.dma_start(
                     out=plane[first_row + r : P : 32, :, :].bitcast(I32),
                     in_=scales[:, r:16:4, :].rearrange("g q n -> q g n").bitcast(I32),
                 )
@@ -110,12 +109,13 @@ def tile_bilateral_grid_affine_k3_kernel(
             load_image(u, "u", u_of, half, first, count)
 
         load_h(0, 2)
+        load_plane(nc.sync, h_plane_first, h_scales[:, :, 0:H_FIRST], 0)
         load_a(0)
-        load_plane(h_plane, h_scales, 0)
-        load_plane(a_plane, a_scales, 0)
-        load_b(0)
+        load_plane(nc.sync, a_plane[0], a_scales[:, :, 0:HALF], 0)
+        load_plane(nc.gpsimd, b_plane, b_scales, B_ROW)
+        load_plane(nc.gpsimd, h_plane_rest, h_scales[:, :, H_FIRST:PIXELS], 0)
         load_x(0, 0, 2)
-        load_plane(b_plane, b_scales, B_ROW)
+        load_b(0)
         load_h(2, 2)
         load_x(0, 2, 2)
         load_c(0, 0)
@@ -131,13 +131,18 @@ def tile_bilateral_grid_affine_k3_kernel(
         load_c(1, 0)
         load_c(1, 1)
         load_a(1)
+        load_plane(nc.sync, a_plane[1], a_scales[:, :, HALF:CHANNELS], 0)
         load_b(1)
         load_x(1, 0, 4)
         load_u(0, 8, 4)
-        for first in range(0, TILES, 4):
-            if first > 0:
-                load_x(1, first, 4)
-            load_u(1, first, 4)
+        load_u(1, 0, 4)
+        load_x(1, 4, 4)
+        load_u(1, 4, 4)
+        load_x(1, 8, 4)
+        load_u(1, 8, 4)
+
+        ident = keep.tile([P, P], F32, name="ident")
+        make_identity(nc, ident[:])
 
         c_lined, c_codes, c_plane = {}, {}, {}
         for half in range(2):
@@ -154,16 +159,6 @@ def tile_bilateral_grid_affine_k3_kernel(
                 in_=c_raw[half, g][:, :, cols].rearrange("p t (c i) -> p c t i", i=4),
             )
 
-        def line_up_c_gpsimd(half, g, cols):
-            nc.gpsimd.tensor_scalar(
-                out=c_lined[half][:, g, cols, :],
-                in0=c_raw[half, g][:, :, cols].rearrange("p t c -> p c t"),
-                scalar1=1.0,
-                scalar2=0.0,
-                op0=MULT,
-                op1=ADD,
-            )
-
         def quantize_c(half, passes):
             nc.vector.quantize_mx(
                 out=c_codes[half][:, passes, :].rearrange("p g n -> p (g n)").bitcast(FP8X4),
@@ -174,12 +169,16 @@ def tile_bilateral_grid_affine_k3_kernel(
         def slice_grid(unit, codes_of_pass, plane_of_pass):
             tile_no = unit % TILES
             h_codes, i = h_of[tile_no]
+            if P * tile_no < H_FIRST:
+                h_plane, first = h_plane_first, P * tile_no
+            else:
+                h_plane, first = h_plane_rest, P * tile_no - H_FIRST
             acc = psum.tile([P, HALF], F32, name="acc", bufs=6)
             for g in range(PASSES):
                 nc.tensor.matmul_mx(
                     out=acc[:],
                     lhsT=h_codes[:, g, P * i : P * (i + 1)].bitcast(FP8X4),
-                    lhsT_scale=h_plane[:, g, P * tile_no : P * (tile_no + 1)],
+                    lhsT_scale=h_plane[:, g, first : first + P],
                     rhs=codes_of_pass(g),
                     rhs_scale=plane_of_pass(g),
                     start=(g == 0),
@@ -189,8 +188,7 @@ def tile_bilateral_grid_affine_k3_kernel(
 
         def job_a(unit):
             half = unit // TILES
-            cols = slice(HALF * half, HALF * (half + 1))
-            acc = slice_grid(unit, lambda g: a_of[half][:, g, :].bitcast(FP4X4), lambda g: a_plane[:, g, cols])
+            acc = slice_grid(unit, lambda g: a_of[half][:, g, :].bitcast(FP4X4), lambda g: a_plane[half][:, g, :])
             nc.vector.tensor_tensor(out=y_of[unit // 2][:, unit % 2, :], in0=acc[:], in1=x_of[unit], op=MULT)
 
         def job_b(unit):
@@ -257,18 +255,19 @@ def tile_bilateral_grid_affine_k3_kernel(
                 in_=codes[:].bitcast(I32),
             )
 
-        def store_plane(half):
+        def store_plane(half, cols, queue):
             for r in range(4):
-                nc.sync.dma_start(
-                    out=out_2[half, r:16:4, :].bitcast(I32), in_=y_plane[half][r:P:32, :].bitcast(I32)
+                queue.dma_start(
+                    out=out_2[half, r:16:4, cols].bitcast(I32), in_=y_plane[half][r:P:32, cols].bitcast(I32)
                 )
 
         left, right = slice(0, HALF // 2), slice(HALF // 2, HALF)
         both = slice(0, 2)
 
-        for g in range(PASSES):
-            line_up_c_scalar(0, g, left)
-            line_up_c_gpsimd(0, g, right)
+        line_up_c_scalar(0, 0, left)
+        line_up_c_scalar(0, 0, right)
+        line_up_c_scalar(0, 1, left)
+        line_up_c_scalar(0, 1, right)
         for pair in range(3):
             job_a(2 * pair)
             job_a(2 * pair + 1)
@@ -287,34 +286,37 @@ def tile_bilateral_grid_affine_k3_kernel(
                 lined = work.tile([P, 2, 4 * 2 * P], BF16, name="y_lined", bufs=2, align_bytes=64)
                 for j in range(2):
                     empty_bank(banks[j], lined[:, j, :], nc.scalar.copy)
-            if 2 <= pair <= 5:
+            if 2 <= pair < 6:
                 g, side = divmod(pair - 2, 2)
                 line_up_c_scalar(1, g, (left, right)[side])
             if pair >= 1:
                 round_y(pair - 1, both)
                 store_y(pair - 1, both)
-            if group_due or pair == 5:
+            if pair in (4, 5, 6, 8, 10,):
                 job_a(ahead)
                 job_a(ahead + 1)
                 job_b(ahead)
                 job_b(ahead + 1)
                 ahead = ahead + 2
                 job_c(2 * pair)
-                if group_due:
-                    quantize_y(lined[:].rearrange("p j n -> p (j n)"), pair - 4, 2)
-                    if pair == 8:
-                        store_plane(0)
-                else:
-                    quantize_c(1, both)
             else:
                 job_a(ahead)
                 job_c(2 * pair)
                 job_b(ahead)
                 ahead = ahead + 1
+            if group_due:
+                quantize_y(lined[:].rearrange("p j n -> p (j n)"), pair - 4, 2)
+                if pair == 8:
+                    store_plane(0, slice(0, PIXELS), nc.sync)
+                if pair == 10:
+                    store_plane(1, slice(0, 4 * P), nc.sync)
+            if pair == 5:
+                quantize_c(1, both)
             job_c(2 * pair + 1)
             finish_pair(pair)
             if pair >= 3 and pair % 2 == 1:
                 banks = [turn(pair - 3), turn(pair - 2)]
+        assert ahead == UNITS - 2
 
         last = PAIRS - 1
         job_a(2 * last)
@@ -326,21 +328,33 @@ def tile_bilateral_grid_affine_k3_kernel(
         round_y(last - 1, both)
         store_y(last - 1, both)
         job_b(2 * last)
-        job_b(2 * last + 1)
         job_c(2 * last)
+        job_b(2 * last + 1)
         job_c(2 * last + 1)
         bank_before = turn(last - 1)
-        for i in range(2):
-            y = y_of[last][:, i, :]
-            nc.vector.tensor_tensor(out=y, in0=y, in1=ux_of[last][:, i, :], op=ADD)
-            round_y(last, slice(i, i + 1))
-            store_y(last, slice(i, i + 1))
-        bank_last = turn(last)
         lined_before = work.tile([P, 4 * 2 * P], BF16, name="lined_before", align_bytes=64)
-        lined_last = work.tile([P, 4 * 2 * P], BF16, name="lined_last", align_bytes=64)
+        lined_last = work.tile([P, 2, 4 * P], BF16, name="lined_last", align_bytes=64)
+        tail_banks = []
+        for i, engine in enumerate((nc.gpsimd, nc.vector)):
+            y = y_of[last][:, i, :]
+            engine.tensor_tensor(out=y, in0=y, in1=ux_of[last][:, i, :], op=ADD)
+            rounded = work.tile([P, HALF], BF16, name="y_bf16_last", bufs=2)
+            nc.scalar.copy(
+                out=rounded[:].rearrange("x (w p e) -> x w p e", w=2, e=2),
+                in_=y.rearrange("x (p w e) -> x w p e", w=2, e=2),
+            )
+            store_y(last, slice(i, i + 1))
+            bank = psum.tile([P, 2, P], F32, name="acc", bufs=6)
+            for w in range(2):
+                nc.tensor.transpose(bank[:, w, :], rounded[:].bitcast(F32)[:, P * w : P * (w + 1)], ident[:])
+            tail_banks.append(bank)
         empty_bank(bank_before, lined_before[:], nc.vector.tensor_copy)
-        empty_bank(bank_last, lined_last[:], nc.scalar.copy)
+        for i in range(2):
+            nc.scalar.copy(
+                out=lined_last[:, i, :].bitcast(F32).rearrange("p (m w) -> p m w", w=2),
+                in_=tail_banks[i][:].rearrange("p w m -> p m w"),
+            )
         quantize_y(lined[:].rearrange("p j n -> p (j n)"), last - 3, 2)
         quantize_y(lined_before[:], last - 1, 1)
-        quantize_y(lined_last[:], last, 1)
-        store_plane(1)
+        quantize_y(lined_last[:].rearrange("p i n -> p (i n)"), last, 1)
+        store_plane(1, slice(4 * P, PIXELS), nc.scalar)

@@ -39,8 +39,8 @@ def tile_bilateral_grid_affine_k3_kernel(
         h_plane_first = keep.tile([P, PASSES, H_FIRST], U8, name="h_plane_first", align_bytes=64)
         h_plane_rest = keep.tile([P, PASSES, PIXELS - H_FIRST], U8, name="h_plane_rest", align_bytes=64)
         a_plane = [keep.tile([P, PASSES, HALF], U8, name="a_plane%d" % h, align_bytes=64) for h in range(2)]
-        b_plane = keep.tile([P, PASSES, CHANNELS], U8, name="b_plane", align_bytes=64)
-        for plane in (h_plane_first, b_plane, a_plane[0], h_plane_rest, a_plane[1]):
+        b_plane = [keep.tile([P, PASSES, HALF], U8, name="b_plane%d" % h, align_bytes=64) for h in range(2)]
+        for plane in (h_plane_first, a_plane[0], b_plane[0], h_plane_rest, a_plane[1], b_plane[1]):
             nc.vector.memset(plane[:].bitcast(I32), 0)
 
         h_rows = h_words.rearrange("g p n t -> p g (n t)")
@@ -112,10 +112,9 @@ def tile_bilateral_grid_affine_k3_kernel(
         load_plane(nc.sync, h_plane_first, h_scales[:, :, 0:H_FIRST], 0)
         load_a(0)
         load_plane(nc.sync, a_plane[0], a_scales[:, :, 0:HALF], 0)
-        load_plane(nc.gpsimd, b_plane, b_scales, B_ROW)
-        load_plane(nc.gpsimd, h_plane_rest, h_scales[:, :, H_FIRST:PIXELS], 0)
         load_x(0, 0, 2)
         load_b(0)
+        load_plane(nc.sync, b_plane[0], b_scales[:, :, 0:HALF], B_ROW)
         load_h(2, 2)
         load_x(0, 2, 2)
         load_c(0, 0)
@@ -123,23 +122,25 @@ def tile_bilateral_grid_affine_k3_kernel(
         load_x(0, 4, 2)
         load_c(0, 1)
         load_h(6, 2)
+        load_plane(nc.sync, h_plane_rest, h_scales[:, :, H_FIRST:PIXELS], 0)
         load_x(0, 6, 2)
         load_u(0, 0, 4)
-        load_h(8, 4)
-        load_x(0, 8, 4)
-        load_u(0, 4, 4)
         load_c(1, 0)
+        load_h(8, 2)
+        load_x(0, 8, 2)
         load_c(1, 1)
+        load_u(0, 4, 4)
+        load_h(10, 2)
+        load_x(0, 10, 2)
         load_a(1)
         load_plane(nc.sync, a_plane[1], a_scales[:, :, HALF:CHANNELS], 0)
+        load_plane(nc.sync, b_plane[1], b_scales[:, :, HALF:CHANNELS], B_ROW)
         load_b(1)
         load_x(1, 0, 4)
         load_u(0, 8, 4)
+        load_x(1, 4, 8)
         load_u(1, 0, 4)
-        load_x(1, 4, 4)
-        load_u(1, 4, 4)
-        load_x(1, 8, 4)
-        load_u(1, 8, 4)
+        load_u(1, 4, 8)
 
         ident = keep.tile([P, P], F32, name="ident")
         make_identity(nc, ident[:])
@@ -155,8 +156,18 @@ def tile_bilateral_grid_affine_k3_kernel(
 
         def line_up_c_scalar(half, g, cols):
             nc.scalar.copy(
-                out=c_lined[half][:, g, cols, :].rearrange("p (c i) t -> p c t i", i=4),
-                in_=c_raw[half, g][:, :, cols].rearrange("p t (c i) -> p c t i", i=4),
+                out=c_lined[half][:, g, cols, :],
+                in_=c_raw[half, g][:, :, cols].rearrange("p t c -> p c t"),
+            )
+
+        def line_up_c_gpsimd(half, g, cols):
+            nc.gpsimd.tensor_scalar(
+                out=c_lined[half][:, g, cols, :],
+                in0=c_raw[half, g][:, :, cols].rearrange("p t c -> p c t"),
+                scalar1=1.0,
+                scalar2=0.0,
+                op0=MULT,
+                op1=ADD,
             )
 
         def quantize_c(half, passes):
@@ -193,9 +204,8 @@ def tile_bilateral_grid_affine_k3_kernel(
 
         def job_b(unit):
             half = unit // TILES
-            cols = slice(HALF * half, HALF * (half + 1))
             acc = slice_grid(
-                unit, lambda g: b_of[half][:, g, :].bitcast(FP8X4), lambda g: b_plane[B_ROW:P, g, cols]
+                unit, lambda g: b_of[half][:, g, :].bitcast(FP8X4), lambda g: b_plane[half][B_ROW:P, g, :]
             )
             y = y_of[unit // 2][:, unit % 2, :]
             nc.vector.tensor_tensor(out=y, in0=acc[:], in1=y, op=ADD)
@@ -265,16 +275,15 @@ def tile_bilateral_grid_affine_k3_kernel(
         both = slice(0, 2)
 
         line_up_c_scalar(0, 0, left)
-        line_up_c_scalar(0, 0, right)
+        line_up_c_gpsimd(0, 0, right)
         line_up_c_scalar(0, 1, left)
-        line_up_c_scalar(0, 1, right)
+        line_up_c_gpsimd(0, 1, right)
         for pair in range(3):
             job_a(2 * pair)
             job_a(2 * pair + 1)
-            if pair == 2:
-                quantize_c(0, slice(0, 1))
             job_b(2 * pair)
             job_b(2 * pair + 1)
+        quantize_c(0, slice(0, 1))
         quantize_c(0, slice(1, 2))
 
         ahead = 6
@@ -286,13 +295,12 @@ def tile_bilateral_grid_affine_k3_kernel(
                 lined = work.tile([P, 2, 4 * 2 * P], BF16, name="y_lined", bufs=2, align_bytes=64)
                 for j in range(2):
                     empty_bank(banks[j], lined[:, j, :], nc.scalar.copy)
-            if 2 <= pair < 6:
-                g, side = divmod(pair - 2, 2)
-                line_up_c_scalar(1, g, (left, right)[side])
+            if pair < PASSES:
+                line_up_c_scalar(1, pair, slice(0, HALF))
             if pair >= 1:
                 round_y(pair - 1, both)
                 store_y(pair - 1, both)
-            if pair in (4, 5, 6, 8, 10,):
+            if pair in (2, 4, 6, 8, 10,):
                 job_a(ahead)
                 job_a(ahead + 1)
                 job_b(ahead)
@@ -310,7 +318,7 @@ def tile_bilateral_grid_affine_k3_kernel(
                     store_plane(0, slice(0, PIXELS), nc.sync)
                 if pair == 10:
                     store_plane(1, slice(0, 4 * P), nc.sync)
-            if pair == 5:
+            if pair == 2:
                 quantize_c(1, both)
             job_c(2 * pair + 1)
             finish_pair(pair)

@@ -17,13 +17,21 @@ MULT = mybir.AluOpType.mult
 ADD = mybir.AluOpType.add
 
 P = 128
-PASSES = CELLS // 512
+K_PASS = 4 * P
+PASSES = CELLS // K_PASS
 HALF = 512
 TILES = PIXELS // P
-UNITS = 2 * TILES
-PAIRS = UNITS // 2
+PAIRS = TILES
+PAIR_PIXELS = 2 * P
+PAIR_VALUES = 4 * PAIR_PIXELS
+
 B_ROW = 4
-H_FIRST = 6 * P
+H_FIRST = 8 * P
+HEAD_UNITS = 6
+C_ROUND = 2
+FIRST_Y_ROUND = 4
+HELD_BACK = 64
+JOB_BANKS, TURN_BANKS = 6, 2
 
 
 def tile_bilateral_grid_affine_k3_kernel(
@@ -35,6 +43,9 @@ def tile_bilateral_grid_affine_k3_kernel(
         work = ctx.enter_context(tc.tile_pool(name="work", bufs=1))
         psum = ctx.enter_context(tc.psum_pool(name="psum", bufs=1))
         ctx.enter_context(tc.manual_schedule())
+
+        def channels_of(half):
+            return slice(HALF * half, HALF * (half + 1))
 
         h_plane_first = keep.tile([P, PASSES, H_FIRST], U8, name="h_plane_first", align_bytes=64)
         h_plane_rest = keep.tile([P, PASSES, PIXELS - H_FIRST], U8, name="h_plane_rest", align_bytes=64)
@@ -49,9 +60,9 @@ def tile_bilateral_grid_affine_k3_kernel(
         h_of, x_of, u_of = {}, {}, {}
         a_of, b_of, c_raw = {}, {}, {}
 
-        def load_plane(queue, plane, scales, first_row):
+        def load_plane(plane, scales, first_row):
             for r in range(4):
-                queue.dma_start(
+                nc.sync.dma_start(
                     out=plane[first_row + r : P : 32, :, :].bitcast(I32),
                     in_=scales[:, r:16:4, :].rearrange("g q n -> q g n").bitcast(I32),
                 )
@@ -83,24 +94,18 @@ def tile_bilateral_grid_affine_k3_kernel(
 
         def load_c(half, g):
             raw = keep.tile([P, 4, HALF], BF16, name="c_raw%d%d" % (half, g))
-            nc.sync.dma_start(
-                out=raw[:],
-                in_=c_grid[512 * g : 512 * (g + 1), HALF * half : HALF * (half + 1)].rearrange(
-                    "(p t) n -> p t n", t=4
-                ),
-            )
+            rows = c_grid[K_PASS * g : K_PASS * (g + 1), channels_of(half)]
+            nc.sync.dma_start(out=raw[:], in_=rows.rearrange("(p t) n -> p t n", t=4))
             c_raw[half, g] = raw
 
-        def load_image(image, name, store, half, first, count):
+        def load_image(image, name, unit_of, half, first, count):
             rows = keep.tile([P, count, HALF], BF16, name="%s%d_%d" % (name, half, first))
             nc.sync.dma_start(
                 out=rows[:],
-                in_=image[P * first : P * (first + count), HALF * half : HALF * (half + 1)].rearrange(
-                    "(i p) n -> p i n", p=P
-                ),
+                in_=image[P * first : P * (first + count), channels_of(half)].rearrange("(i p) n -> p i n", p=P),
             )
             for i in range(count):
-                store[TILES * half + first + i] = rows[:, i, :]
+                unit_of[TILES * half + first + i] = rows[:, i, :]
 
         def load_x(half, first, count):
             load_image(x, "x", x_of, half, first, count)
@@ -109,12 +114,12 @@ def tile_bilateral_grid_affine_k3_kernel(
             load_image(u, "u", u_of, half, first, count)
 
         load_h(0, 2)
-        load_plane(nc.sync, h_plane_first, h_scales[:, :, 0:H_FIRST], 0)
+        load_plane(h_plane_first, h_scales[:, :, 0:H_FIRST], 0)
         load_a(0)
-        load_plane(nc.sync, a_plane[0], a_scales[:, :, 0:HALF], 0)
+        load_plane(a_plane[0], a_scales[:, :, channels_of(0)], 0)
         load_x(0, 0, 2)
         load_b(0)
-        load_plane(nc.sync, b_plane[0], b_scales[:, :, 0:HALF], B_ROW)
+        load_plane(b_plane[0], b_scales[:, :, channels_of(0)], B_ROW)
         load_h(2, 2)
         load_x(0, 2, 2)
         load_c(0, 0)
@@ -122,19 +127,19 @@ def tile_bilateral_grid_affine_k3_kernel(
         load_x(0, 4, 2)
         load_c(0, 1)
         load_h(6, 2)
-        load_plane(nc.sync, h_plane_rest, h_scales[:, :, H_FIRST:PIXELS], 0)
         load_x(0, 6, 2)
         load_u(0, 0, 4)
         load_c(1, 0)
         load_h(8, 2)
+        load_plane(h_plane_rest, h_scales[:, :, H_FIRST:PIXELS], 0)
         load_x(0, 8, 2)
         load_c(1, 1)
         load_u(0, 4, 4)
         load_h(10, 2)
         load_x(0, 10, 2)
         load_a(1)
-        load_plane(nc.sync, a_plane[1], a_scales[:, :, HALF:CHANNELS], 0)
-        load_plane(nc.sync, b_plane[1], b_scales[:, :, HALF:CHANNELS], B_ROW)
+        load_plane(a_plane[1], a_scales[:, :, channels_of(1)], 0)
+        load_plane(b_plane[1], b_scales[:, :, channels_of(1)], B_ROW)
         load_b(1)
         load_x(1, 0, 4)
         load_u(0, 8, 4)
@@ -152,7 +157,7 @@ def tile_bilateral_grid_affine_k3_kernel(
             c_plane[half] = keep.tile([P, PASSES, HALF], U8, name="c_plane%d" % half, align_bytes=64)
         y_of = [keep.tile([P, 2, HALF], F32, name="y%d" % pair) for pair in range(PAIRS)]
         y_plane = [keep.tile([P, PIXELS], U8, name="y_plane%d" % half, align_bytes=64) for half in range(2)]
-        ux_of, yb_of = {}, {}
+        su_u_of, y_bf16_of = {}, {}
 
         def line_up_c_scalar(half, g, cols):
             nc.scalar.copy(
@@ -181,15 +186,15 @@ def tile_bilateral_grid_affine_k3_kernel(
             tile_no = unit % TILES
             h_codes, i = h_of[tile_no]
             if P * tile_no < H_FIRST:
-                h_plane, first = h_plane_first, P * tile_no
+                h_plane, column = h_plane_first, P * tile_no
             else:
-                h_plane, first = h_plane_rest, P * tile_no - H_FIRST
-            acc = psum.tile([P, HALF], F32, name="acc", bufs=6)
+                h_plane, column = h_plane_rest, P * tile_no - H_FIRST
+            acc = psum.tile([P, HALF], F32, name="acc", bufs=JOB_BANKS)
             for g in range(PASSES):
                 nc.tensor.matmul_mx(
                     out=acc[:],
                     lhsT=h_codes[:, g, P * i : P * (i + 1)].bitcast(FP8X4),
-                    lhsT_scale=h_plane[:, g, first : first + P],
+                    lhsT_scale=h_plane[:, g, column : column + P],
                     rhs=codes_of_pass(g),
                     rhs_scale=plane_of_pass(g),
                     start=(g == 0),
@@ -210,36 +215,43 @@ def tile_bilateral_grid_affine_k3_kernel(
             y = y_of[unit // 2][:, unit % 2, :]
             nc.vector.tensor_tensor(out=y, in0=acc[:], in1=y, op=ADD)
 
-        def job_c(unit):
+        def job_c(unit, quantize=None):
             half = unit // TILES
             if unit % 2 == 0:
-                ux_of[unit // 2] = work.tile([P, 2, HALF], F32, name="su_u", bufs=3)
+                su_u_of[unit // 2] = work.tile([P, 2, HALF], F32, name="su_u", bufs=4)
             acc = slice_grid(unit, lambda g: c_codes[half][:, g, :].bitcast(FP8X4), lambda g: c_plane[half][:, g, :])
-            nc.vector.tensor_tensor(out=ux_of[unit // 2][:, unit % 2, :], in0=acc[:], in1=u_of[unit], op=MULT)
+            su_u = su_u_of[unit // 2][:, unit % 2, :]
+            if quantize is None:
+                nc.vector.tensor_tensor(out=su_u, in0=acc[:], in1=u_of[unit], op=MULT)
+            else:
+                most, rest = slice(0, HALF - HELD_BACK), slice(HALF - HELD_BACK, HALF)
+                nc.vector.tensor_tensor(out=su_u[:, most], in0=acc[:, most], in1=u_of[unit][:, most], op=MULT)
+                quantize()
+                nc.vector.tensor_tensor(out=su_u[:, rest], in0=acc[:, rest], in1=u_of[unit][:, rest], op=MULT)
 
         def finish_pair(pair):
             y = y_of[pair][:].rearrange("p i n -> p (i n)")
-            nc.gpsimd.tensor_tensor(out=y, in0=y, in1=ux_of[pair][:].rearrange("p i n -> p (i n)"), op=ADD)
+            nc.gpsimd.tensor_tensor(out=y, in0=y, in1=su_u_of[pair][:].rearrange("p i n -> p (i n)"), op=ADD)
 
         def store_y(pair, members):
             half, first = divmod(2 * pair, TILES)
-            rows = out_0[P * first : P * (first + 2), HALF * half : HALF * (half + 1)].rearrange(
-                "(i p) n -> p i n", p=P
-            )
+            rows = out_0[P * first : P * (first + 2), channels_of(half)].rearrange("(i p) n -> p i n", p=P)
             nc.sync.dma_start(out=rows[:, members, :], in_=y_of[pair][:, members, :])
 
-        def round_y(pair, members):
-            if members.start == 0:
-                yb_of[pair] = work.tile([P, 2, HALF], BF16, name="y_bf16", bufs=4)
-            for i in range(members.start, members.stop):
-                nc.scalar.copy(
-                    out=yb_of[pair][:, i, :].rearrange("x (w p e) -> x w p e", w=2, e=2),
-                    in_=y_of[pair][:, i, :].rearrange("x (p w e) -> x w p e", w=2, e=2),
-                )
+        def round_unit(rounded, y):
+            nc.scalar.copy(
+                out=rounded.rearrange("m (w p e) -> m w p e", w=2, e=2),
+                in_=y.rearrange("m (p w e) -> m w p e", w=2, e=2),
+            )
 
-        def turn(pair):
-            bank = psum.tile([P, 2, 2, P], F32, name="turned", bufs=2)
-            words = yb_of[pair][:].bitcast(F32)
+        def round_pair(pair):
+            y_bf16_of[pair] = work.tile([P, 2, HALF], BF16, name="y_bf16", bufs=4)
+            for i in range(2):
+                round_unit(y_bf16_of[pair][:, i, :], y_of[pair][:, i, :])
+
+        def turn_pair(pair):
+            bank = psum.tile([P, 2, 2, P], F32, name="turned", bufs=TURN_BANKS)
+            words = y_bf16_of[pair][:].bitcast(F32)
             for i in range(2):
                 for w in range(2):
                     nc.tensor.transpose(bank[:, i, w, :], words[:, i, P * w : P * (w + 1)], ident[:])
@@ -251,118 +263,115 @@ def tile_bilateral_grid_affine_k3_kernel(
                 in_=bank[:].rearrange("p i w m -> p i m w"),
             )
 
+        def empty_two_banks(banks):
+            lined = work.tile([P, 2, PAIR_VALUES], BF16, name="y_lined", bufs=2, align_bytes=64)
+            for j in range(2):
+                empty_bank(banks[j], lined[:, j, :], nc.scalar.copy)
+            return lined[:].rearrange("p j n -> p (j n)")
+
         def quantize_y(lined, first_pair, pairs):
             half, first = divmod(2 * first_pair, TILES)
-            width = 2 * P * pairs
+            pixel, width = P * first, PAIR_PIXELS * pairs
             codes = keep.tile([P, width], U32, name="y_codes%d" % first_pair, align_bytes=64)
             nc.vector.quantize_mx(
-                out=codes[:].bitcast(FP8X4),
-                scales=y_plane[half][:, P * first : P * first + width],
-                in_=lined,
+                out=codes[:].bitcast(FP8X4), scales=y_plane[half][:, pixel : pixel + width], in_=lined
             )
             nc.sync.dma_start(
-                out=out_1[half].rearrange("p m t -> p (m t)")[:, 4 * P * first : 4 * (P * first + width)].bitcast(I32),
+                out=out_1[half].rearrange("p m t -> p (m t)")[:, 4 * pixel : 4 * (pixel + width)].bitcast(I32),
                 in_=codes[:].bitcast(I32),
             )
 
-        def store_plane(half, cols, queue):
+        def store_plane(half, pixels, queue):
             for r in range(4):
                 queue.dma_start(
-                    out=out_2[half, r:16:4, cols].bitcast(I32), in_=y_plane[half][r:P:32, cols].bitcast(I32)
+                    out=out_2[half, r:16:4, pixels].bitcast(I32), in_=y_plane[half][r:P:32, pixels].bitcast(I32)
                 )
 
-        left, right = slice(0, HALF // 2), slice(HALF // 2, HALF)
         both = slice(0, 2)
 
-        line_up_c_scalar(0, 0, left)
-        line_up_c_gpsimd(0, 0, right)
-        line_up_c_scalar(0, 1, left)
-        line_up_c_gpsimd(0, 1, right)
-        for pair in range(3):
-            job_a(2 * pair)
-            job_a(2 * pair + 1)
-            job_b(2 * pair)
-            job_b(2 * pair + 1)
-        quantize_c(0, slice(0, 1))
-        quantize_c(0, slice(1, 2))
+        for g in range(PASSES):
+            line_up_c_scalar(0, g, slice(0, HALF // 2))
+            line_up_c_gpsimd(0, g, slice(HALF // 2, HALF))
+        for unit in range(0, HEAD_UNITS, 2):
+            job_a(unit)
+            job_a(unit + 1)
+            job_b(unit)
+            job_b(unit + 1)
+        for g in range(PASSES):
+            quantize_c(0, slice(g, g + 1))
 
-        ahead = 6
-        banks = []
-        lined = None
-        for pair in range(PAIRS - 1):
-            group_due = pair >= 4 and pair % 2 == 0
-            if group_due:
-                lined = work.tile([P, 2, 4 * 2 * P], BF16, name="y_lined", bufs=2, align_bytes=64)
-                for j in range(2):
-                    empty_bank(banks[j], lined[:, j, :], nc.scalar.copy)
-            if pair < PASSES:
-                line_up_c_scalar(1, pair, slice(0, HALF))
-            if pair >= 1:
-                round_y(pair - 1, both)
-                store_y(pair - 1, both)
-            if pair in (2, 4, 6, 8, 10,):
+        ahead = HEAD_UNITS
+        banks, lined = None, None
+        last = PAIRS - 1
+        for r in range(last):
+            y_round = r >= FIRST_Y_ROUND and r % 2 == 0
+            if y_round:
+                lined = empty_two_banks(banks)
+            if r < PASSES:
+                line_up_c_scalar(1, r, slice(0, HALF))
+            if r >= 2 and r % 2 == 0:
+                round_pair(r - 2)
+                round_pair(r - 1)
+            if r >= 1:
+                store_y(r - 1, both)
+            if r == 0 or y_round:
                 job_a(ahead)
                 job_a(ahead + 1)
                 job_b(ahead)
                 job_b(ahead + 1)
                 ahead = ahead + 2
-                job_c(2 * pair)
+                job_c(2 * r)
             else:
                 job_a(ahead)
-                job_c(2 * pair)
+                job_c(2 * r)
                 job_b(ahead)
                 ahead = ahead + 1
-            if group_due:
-                quantize_y(lined[:].rearrange("p j n -> p (j n)"), pair - 4, 2)
-                if pair == 8:
+            if y_round:
+                first_pair = r - FIRST_Y_ROUND
+                job_c(2 * r + 1, lambda: quantize_y(lined, first_pair, 2))
+                if first_pair + 2 == PAIRS // 2:
                     store_plane(0, slice(0, PIXELS), nc.sync)
-                if pair == 10:
-                    store_plane(1, slice(0, 4 * P), nc.sync)
-            if pair == 2:
-                quantize_c(1, both)
-            job_c(2 * pair + 1)
-            finish_pair(pair)
-            if pair >= 3 and pair % 2 == 1:
-                banks = [turn(pair - 3), turn(pair - 2)]
-        assert ahead == UNITS - 2
+                if first_pair == PAIRS // 2:
+                    store_plane(1, slice(0, 2 * PAIR_PIXELS), nc.sync)
+            elif r == C_ROUND:
+                job_c(2 * r + 1, lambda: quantize_c(1, both))
+            else:
+                job_c(2 * r + 1)
+            finish_pair(r)
+            if r >= FIRST_Y_ROUND - 1 and r % 2 == 1:
+                banks = [turn_pair(r - 3), turn_pair(r - 2)]
+        assert ahead == 2 * last
 
-        last = PAIRS - 1
         job_a(2 * last)
         job_a(2 * last + 1)
-        banks = [turn(last - 3), turn(last - 2)]
-        lined = work.tile([P, 2, 4 * 2 * P], BF16, name="y_lined", bufs=2, align_bytes=64)
-        for j in range(2):
-            empty_bank(banks[j], lined[:, j, :], nc.scalar.copy)
-        round_y(last - 1, both)
-        store_y(last - 1, both)
         job_b(2 * last)
+        lined = empty_two_banks([turn_pair(last - 3), turn_pair(last - 2)])
+        round_pair(last - 1)
+        store_y(last - 1, both)
         job_c(2 * last)
         job_b(2 * last + 1)
         job_c(2 * last + 1)
-        bank_before = turn(last - 1)
-        lined_before = work.tile([P, 4 * 2 * P], BF16, name="lined_before", align_bytes=64)
-        lined_last = work.tile([P, 2, 4 * P], BF16, name="lined_last", align_bytes=64)
-        tail_banks = []
+        bank_before = turn_pair(last - 1)
+        lined_before = work.tile([P, PAIR_VALUES], BF16, name="lined_before", align_bytes=64)
+        lined_last = work.tile([P, 2, PAIR_VALUES // 2], BF16, name="lined_last", align_bytes=64)
+        last_banks = []
         for i, engine in enumerate((nc.gpsimd, nc.vector)):
             y = y_of[last][:, i, :]
-            engine.tensor_tensor(out=y, in0=y, in1=ux_of[last][:, i, :], op=ADD)
+            engine.tensor_tensor(out=y, in0=y, in1=su_u_of[last][:, i, :], op=ADD)
             rounded = work.tile([P, HALF], BF16, name="y_bf16_last", bufs=2)
-            nc.scalar.copy(
-                out=rounded[:].rearrange("x (w p e) -> x w p e", w=2, e=2),
-                in_=y.rearrange("x (p w e) -> x w p e", w=2, e=2),
-            )
+            round_unit(rounded[:], y)
             store_y(last, slice(i, i + 1))
-            bank = psum.tile([P, 2, P], F32, name="acc", bufs=6)
+            bank = psum.tile([P, 2, P], F32, name="acc", bufs=JOB_BANKS)
             for w in range(2):
                 nc.tensor.transpose(bank[:, w, :], rounded[:].bitcast(F32)[:, P * w : P * (w + 1)], ident[:])
-            tail_banks.append(bank)
+            last_banks.append(bank)
         empty_bank(bank_before, lined_before[:], nc.vector.tensor_copy)
         for i in range(2):
             nc.scalar.copy(
                 out=lined_last[:, i, :].bitcast(F32).rearrange("p (m w) -> p m w", w=2),
-                in_=tail_banks[i][:].rearrange("p w m -> p m w"),
+                in_=last_banks[i][:].rearrange("p w m -> p m w"),
             )
-        quantize_y(lined[:].rearrange("p j n -> p (j n)"), last - 3, 2)
+        quantize_y(lined, last - 3, 2)
         quantize_y(lined_before[:], last - 1, 1)
         quantize_y(lined_last[:].rearrange("p i n -> p (i n)"), last, 1)
-        store_plane(1, slice(4 * P, PIXELS), nc.scalar)
+        store_plane(1, slice(2 * PAIR_PIXELS, PIXELS), nc.scalar)

@@ -314,7 +314,16 @@ def tile_bilateral_grid_affine_k3_kernel(
                 round_pair(r - 1)
             if r >= 1:
                 store_y(r - 1, both)
-            if r == 0 or y_round:
+            if r == 0:
+                job_a(ahead)
+                job_a(ahead + 1)
+                job_c(2 * r)
+            elif r == 1:
+                job_b(ahead)
+                job_c(2 * r)
+                job_b(ahead + 1)
+                ahead = ahead + 2
+            elif r == C_ROUND or y_round:
                 job_a(ahead)
                 job_a(ahead + 1)
                 job_b(ahead)

from contextlib import ExitStack

import concourse.mybir as mybir
from concourse.masks import make_identity

PIXELS, CELLS, CHANNELS = 1536, 1024, 1024
FLOPS = 2 * 3 * PIXELS * CELLS * CHANNELS

F32 = mybir.dt.float32
BF16 = mybir.dt.bfloat16
I32 = mybir.dt.int32
U32 = mybir.dt.uint32
U8 = mybir.dt.uint8
FP8X4 = mybir.dt.float8_e4m3fn_x4
FP4X4 = mybir.dt.float4_e2m1fn_x4
MULT = mybir.AluOpType.mult
ADD = mybir.AluOpType.add

P = 128
K_PASS = 4 * P
PASSES = CELLS // K_PASS
HALF = 512
TILES = PIXELS // P
PAIRS = TILES
PAIR_PIXELS = 2 * P
PAIR_VALUES = 4 * PAIR_PIXELS

B_ROW = 4
H_FIRST = 8 * P
HEAD_UNITS = 6
C_ROUND = 2
FIRST_Y_ROUND = 4
HELD_BACK = 64
JOB_BANKS, TURN_BANKS = 6, 2


def tile_bilateral_grid_affine_k3_kernel(
    tc, h_words, h_scales, a_words, a_scales, b_words, b_scales, c_grid, x, u, out_0, out_1, out_2
):
    nc = tc.nc
    with ExitStack() as ctx:
        keep = ctx.enter_context(tc.tile_pool(name="keep", bufs=1))
        work = ctx.enter_context(tc.tile_pool(name="work", bufs=1))
        psum = ctx.enter_context(tc.psum_pool(name="psum", bufs=1))
        ctx.enter_context(tc.manual_schedule())

        def channels_of(half):
            return slice(HALF * half, HALF * (half + 1))

        h_plane_first = keep.tile([P, PASSES, H_FIRST], U8, name="h_plane_first", align_bytes=64)
        h_plane_rest = keep.tile([P, PASSES, PIXELS - H_FIRST], U8, name="h_plane_rest", align_bytes=64)
        a_plane = [keep.tile([P, PASSES, HALF], U8, name="a_plane%d" % h, align_bytes=64) for h in range(2)]
        b_plane = [keep.tile([P, PASSES, HALF], U8, name="b_plane%d" % h, align_bytes=64) for h in range(2)]
        for plane in (h_plane_first, a_plane[0], b_plane[0], h_plane_rest, a_plane[1], b_plane[1]):
            nc.vector.memset(plane[:].bitcast(I32), 0)

        h_rows = h_words.rearrange("g p n t -> p g (n t)")
        a_rows = a_words.rearrange("g p n -> p g n")
        b_rows = b_words.rearrange("g p n t -> p g (n t)")
        h_of, x_of, u_of = {}, {}, {}
        a_of, b_of, c_raw = {}, {}, {}

        def load_plane(plane, scales, first_row):
            for r in range(4):
                nc.sync.dma_start(
                    out=plane[first_row + r : P : 32, :, :].bitcast(I32),
                    in_=scales[:, r:16:4, :].rearrange("g q n -> q g n").bitcast(I32),
                )

        def load_h(first, count):
            codes = keep.tile([P, PASSES, count * P], U32, name="h%d" % first, align_bytes=64)
            nc.sync.dma_start(
                out=codes[:].bitcast(I32),
                in_=h_rows[:, :, 4 * P * first : 4 * P * (first + count)].bitcast(I32),
            )
            for i in range(count):
                h_of[first + i] = (codes, i)

        def load_a(half):
            codes = keep.tile([P, PASSES, 2 * HALF], U8, name="a%d" % half, align_bytes=64)
            nc.sync.dma_start(
                out=codes[:].bitcast(I32),
                in_=a_rows[:, :, 2 * HALF * half : 2 * HALF * (half + 1)].bitcast(I32),
            )
            a_of[half] = codes

        def load_b(half):
            codes = keep.tile([P, PASSES, HALF], U32, name="b%d" % half, align_bytes=64)
            nc.sync.dma_start(
                out=codes[:].bitcast(I32),
                in_=b_rows[:, :, 4 * HALF * half : 4 * HALF * (half + 1)].bitcast(I32),
            )
            b_of[half] = codes

        def load_c(half, g):
            raw = keep.tile([P, 4, HALF], BF16, name="c_raw%d%d" % (half, g))
            rows = c_grid[K_PASS * g : K_PASS * (g + 1), channels_of(half)]
            nc.sync.dma_start(out=raw[:], in_=rows.rearrange("(p t) n -> p t n", t=4))
            c_raw[half, g] = raw

        def load_image(image, name, unit_of, half, first, count):
            rows = keep.tile([P, count, HALF], BF16, name="%s%d_%d" % (name, half, first))
            nc.sync.dma_start(
                out=rows[:],
                in_=image[P * first : P * (first + count), channels_of(half)].rearrange("(i p) n -> p i n", p=P),
            )
            for i in range(count):
                unit_of[TILES * half + first + i] = rows[:, i, :]

        def load_x(half, first, count):
            load_image(x, "x", x_of, half, first, count)

        def load_u(half, first, count):
            load_image(u, "u", u_of, half, first, count)

        load_h(0, 2)
        load_plane(h_plane_first, h_scales[:, :, 0:H_FIRST], 0)
        load_a(0)
        load_plane(a_plane[0], a_scales[:, :, channels_of(0)], 0)
        load_x(0, 0, 2)
        load_b(0)
        load_plane(b_plane[0], b_scales[:, :, channels_of(0)], B_ROW)
        load_h(2, 2)
        load_x(0, 2, 2)
        load_c(0, 0)
        load_h(4, 2)
        load_x(0, 4, 2)
        load_c(0, 1)
        load_h(6, 2)
        load_x(0, 6, 2)
        load_u(0, 0, 4)
        load_c(1, 0)
        load_h(8, 2)
        load_plane(h_plane_rest, h_scales[:, :, H_FIRST:PIXELS], 0)
        load_x(0, 8, 2)
        load_c(1, 1)
        load_u(0, 4, 4)
        load_h(10, 2)
        load_x(0, 10, 2)
        load_a(1)
        load_plane(a_plane[1], a_scales[:, :, channels_of(1)], 0)
        load_plane(b_plane[1], b_scales[:, :, channels_of(1)], B_ROW)
        load_b(1)
        load_x(1, 0, 4)
        load_u(0, 8, 4)
        load_x(1, 4, 8)
        load_u(1, 0, 4)
        load_u(1, 4, 8)

        ident = keep.tile([P, P], F32, name="ident")
        make_identity(nc, ident[:])

        c_lined, c_codes, c_plane = {}, {}, {}
        for half in range(2):
            c_lined[half] = keep.tile([P, PASSES, HALF, 4], BF16, name="c_lined%d" % half, align_bytes=64)
            c_codes[half] = keep.tile([P, PASSES, HALF], U32, name="c_codes%d" % half, align_bytes=64)
            c_plane[half] = keep.tile([P, PASSES, HALF], U8, name="c_plane%d" % half, align_bytes=64)
        y_of = [keep.tile([P, 2, HALF], F32, name="y%d" % pair) for pair in range(PAIRS)]
        y_plane = [keep.tile([P, PIXELS], U8, name="y_plane%d" % half, align_bytes=64) for half in range(2)]
        su_u_of, y_bf16_of = {}, {}

        def line_up_c_scalar(half, g, cols):
            nc.scalar.copy(
                out=c_lined[half][:, g, cols, :],
                in_=c_raw[half, g][:, :, cols].rearrange("p t c -> p c t"),
            )

        def line_up_c_gpsimd(half, g, cols):
            nc.gpsimd.tensor_scalar(
                out=c_lined[half][:, g, cols, :],
                in0=c_raw[half, g][:, :, cols].rearrange("p t c -> p c t"),
                scalar1=1.0,
                scalar2=0.0,
                op0=MULT,
                op1=ADD,
            )

        def quantize_c(half, passes):
            nc.vector.quantize_mx(
                out=c_codes[half][:, passes, :].rearrange("p g n -> p (g n)").bitcast(FP8X4),
                scales=c_plane[half][:, passes, :].rearrange("p g n -> p (g n)"),
                in_=c_lined[half][:, passes, :, :].rearrange("p g n t -> p (g n t)"),
            )

        def slice_grid(unit, codes_of_pass, plane_of_pass):
            tile_no = unit % TILES
            h_codes, i = h_of[tile_no]
            if P * tile_no < H_FIRST:
                h_plane, column = h_plane_first, P * tile_no
            else:
                h_plane, column = h_plane_rest, P * tile_no - H_FIRST
            acc = psum.tile([P, HALF], F32, name="acc", bufs=JOB_BANKS)
            for g in range(PASSES):
                nc.tensor.matmul_mx(
                    out=acc[:],
                    lhsT=h_codes[:, g, P * i : P * (i + 1)].bitcast(FP8X4),
                    lhsT_scale=h_plane[:, g, column : column + P],
                    rhs=codes_of_pass(g),
                    rhs_scale=plane_of_pass(g),
                    start=(g == 0),
                    stop=(g == PASSES - 1),
                )
            return acc

        def job_a(unit):
            half = unit // TILES
            acc = slice_grid(unit, lambda g: a_of[half][:, g, :].bitcast(FP4X4), lambda g: a_plane[half][:, g, :])
            nc.vector.tensor_tensor(out=y_of[unit // 2][:, unit % 2, :], in0=acc[:], in1=x_of[unit], op=MULT)

        def job_b(unit):
            half = unit // TILES
            acc = slice_grid(
                unit, lambda g: b_of[half][:, g, :].bitcast(FP8X4), lambda g: b_plane[half][B_ROW:P, g, :]
            )
            y = y_of[unit // 2][:, unit % 2, :]
            nc.vector.tensor_tensor(out=y, in0=acc[:], in1=y, op=ADD)

        def job_c(unit, quantize=None):
            half = unit // TILES
            if unit % 2 == 0:
                su_u_of[unit // 2] = work.tile([P, 2, HALF], F32, name="su_u", bufs=4)
            acc = slice_grid(unit, lambda g: c_codes[half][:, g, :].bitcast(FP8X4), lambda g: c_plane[half][:, g, :])
            su_u = su_u_of[unit // 2][:, unit % 2, :]
            if quantize is None:
                nc.vector.tensor_tensor(out=su_u, in0=acc[:], in1=u_of[unit], op=MULT)
            else:
                most, rest = slice(0, HALF - HELD_BACK), slice(HALF - HELD_BACK, HALF)
                nc.vector.tensor_tensor(out=su_u[:, most], in0=acc[:, most], in1=u_of[unit][:, most], op=MULT)
                quantize()
                nc.vector.tensor_tensor(out=su_u[:, rest], in0=acc[:, rest], in1=u_of[unit][:, rest], op=MULT)

        def finish_pair(pair):
            y = y_of[pair][:].rearrange("p i n -> p (i n)")
            nc.gpsimd.tensor_tensor(out=y, in0=y, in1=su_u_of[pair][:].rearrange("p i n -> p (i n)"), op=ADD)

        def store_y(pair, members):
            half, first = divmod(2 * pair, TILES)
            rows = out_0[P * first : P * (first + 2), channels_of(half)].rearrange("(i p) n -> p i n", p=P)
            nc.sync.dma_start(out=rows[:, members, :], in_=y_of[pair][:, members, :])

        def round_unit(rounded, y):
            nc.scalar.copy(
                out=rounded.rearrange("m (w p e) -> m w p e", w=2, e=2),
                in_=y.rearrange("m (p w e) -> m w p e", w=2, e=2),
            )

        def round_pair(pair):
            y_bf16_of[pair] = work.tile([P, 2, HALF], BF16, name="y_bf16", bufs=4)
            for i in range(2):
                round_unit(y_bf16_of[pair][:, i, :], y_of[pair][:, i, :])

        def turn_pair(pair):
            bank = psum.tile([P, 2, 2, P], F32, name="turned", bufs=TURN_BANKS)
            words = y_bf16_of[pair][:].bitcast(F32)
            for i in range(2):
                for w in range(2):
                    nc.tensor.transpose(bank[:, i, w, :], words[:, i, P * w : P * (w + 1)], ident[:])
            return bank

        def empty_bank(bank, lined, copy):
            copy(
                out=lined.bitcast(F32).rearrange("p (i m w) -> p i m w", i=2, w=2),
                in_=bank[:].rearrange("p i w m -> p i m w"),
            )

        def empty_two_banks(banks):
            lined = work.tile([P, 2, PAIR_VALUES], BF16, name="y_lined", bufs=2, align_bytes=64)
            for j in range(2):
                empty_bank(banks[j], lined[:, j, :], nc.scalar.copy)
            return lined[:].rearrange("p j n -> p (j n)")

        def quantize_y(lined, first_pair, pairs):
            half, first = divmod(2 * first_pair, TILES)
            pixel, width = P * first, PAIR_PIXELS * pairs
            codes = keep.tile([P, width], U32, name="y_codes%d" % first_pair, align_bytes=64)
            nc.vector.quantize_mx(
                out=codes[:].bitcast(FP8X4), scales=y_plane[half][:, pixel : pixel + width], in_=lined
            )
            nc.sync.dma_start(
                out=out_1[half].rearrange("p m t -> p (m t)")[:, 4 * pixel : 4 * (pixel + width)].bitcast(I32),
                in_=codes[:].bitcast(I32),
            )

        def store_plane(half, pixels, queue):
            for r in range(4):
                queue.dma_start(
                    out=out_2[half, r:16:4, pixels].bitcast(I32), in_=y_plane[half][r:P:32, pixels].bitcast(I32)
                )

        both = slice(0, 2)

        for g in range(PASSES):
            line_up_c_scalar(0, g, slice(0, HALF // 2))
            line_up_c_gpsimd(0, g, slice(HALF // 2, HALF))
        for unit in range(0, HEAD_UNITS, 2):
            job_a(unit)
            job_a(unit + 1)
            job_b(unit)
            job_b(unit + 1)
        for g in range(PASSES):
            quantize_c(0, slice(g, g + 1))

        ahead = HEAD_UNITS
        banks, lined = None, None
        last = PAIRS - 1
        for r in range(last):
            y_round = r >= FIRST_Y_ROUND and r % 2 == 0
            if y_round:
                lined = empty_two_banks(banks)
            if r < PASSES:
                line_up_c_scalar(1, r, slice(0, HALF))
            if r >= 2 and r % 2 == 0:
                round_pair(r - 2)
                round_pair(r - 1)
            if r >= 1:
                store_y(r - 1, both)
            if r == 0:
                job_a(ahead)
                job_a(ahead + 1)
                job_c(2 * r)
            elif r == 1:
                job_b(ahead)
                job_c(2 * r)
                job_b(ahead + 1)
                ahead = ahead + 2
            elif r == C_ROUND or y_round:
                job_a(ahead)
                job_a(ahead + 1)
                job_b(ahead)
                job_b(ahead + 1)
                ahead = ahead + 2
                job_c(2 * r)
            else:
                job_a(ahead)
                job_c(2 * r)
                job_b(ahead)
                ahead = ahead + 1
            if y_round:
                first_pair = r - FIRST_Y_ROUND
                job_c(2 * r + 1, lambda: quantize_y(lined, first_pair, 2))
                if first_pair + 2 == PAIRS // 2:
                    store_plane(0, slice(0, PIXELS), nc.sync)
                if first_pair == PAIRS // 2:
                    store_plane(1, slice(0, 2 * PAIR_PIXELS), nc.sync)
            elif r == C_ROUND:
                job_c(2 * r + 1, lambda: quantize_c(1, both))
            else:
                job_c(2 * r + 1)
            finish_pair(r)
            if r >= FIRST_Y_ROUND - 1 and r % 2 == 1:
                banks = [turn_pair(r - 3), turn_pair(r - 2)]
        assert ahead == 2 * last

        job_a(2 * last)
        job_a(2 * last + 1)
        job_b(2 * last)
        lined = empty_two_banks([turn_pair(last - 3), turn_pair(last - 2)])
        round_pair(last - 1)
        store_y(last - 1, both)
        job_c(2 * last)
        job_b(2 * last + 1)
        job_c(2 * last + 1)
        bank_before = turn_pair(last - 1)
        lined_before = work.tile([P, PAIR_VALUES], BF16, name="lined_before", align_bytes=64)
        lined_last = work.tile([P, 2, PAIR_VALUES // 2], BF16, name="lined_last", align_bytes=64)
        last_banks = []
        for i, engine in enumerate((nc.gpsimd, nc.vector)):
            y = y_of[last][:, i, :]
            engine.tensor_tensor(out=y, in0=y, in1=su_u_of[last][:, i, :], op=ADD)
            rounded = work.tile([P, HALF], BF16, name="y_bf16_last", bufs=2)
            round_unit(rounded[:], y)
            store_y(last, slice(i, i + 1))
            bank = psum.tile([P, 2, P], F32, name="acc", bufs=JOB_BANKS)
            for w in range(2):
                nc.tensor.transpose(bank[:, w, :], rounded[:].bitcast(F32)[:, P * w : P * (w + 1)], ident[:])
            last_banks.append(bank)
        empty_bank(bank_before, lined_before[:], nc.vector.tensor_copy)
        for i in range(2):
            nc.scalar.copy(
                out=lined_last[:, i, :].bitcast(F32).rearrange("p (m w) -> p m w", w=2),
                in_=last_banks[i][:].rearrange("p w m -> p m w"),
            )
        quantize_y(lined, last - 3, 2)
        quantize_y(lined_before[:], last - 1, 1)
        quantize_y(lined_last[:].rearrange("p i n -> p (i n)"), last, 1)
        store_plane(1, slice(2 * PAIR_PIXELS, PIXELS), nc.scalar)
